import numpy as np
import ml_dtypes


def mxq(x, axis, fmt="e4m3"):
    dtype, down = {"e4m3": (ml_dtypes.float8_e4m3fn, 7), "e5m2": (ml_dtypes.float8_e5m2, 14)}[fmt]
    v = np.moveaxis(np.asarray(x, np.float32).astype(ml_dtypes.bfloat16).astype(np.float64), axis, -1)
    blocks = v.reshape(v.shape[:-1] + (-1, 32))
    amax = np.abs(blocks).max(-1, keepdims=True)
    byte = np.maximum(np.where(amax > 0, np.frexp(amax)[1] - 1 + 127, 0) - down, 1)
    scale = np.exp2(byte - 127.0)
    codes = (blocks / scale).astype(np.float32).astype(dtype).astype(np.float64)
    return np.moveaxis((codes * scale).reshape(v.shape), -1, axis)


WIDE = False


def mx_kscale(k):
    if not WIDE:
        return np.ones(k)
    levels = np.array([10, -10, 5, -5, 0])
    if k % 512:
        return np.exp2(np.random.permutation(np.resize(levels, k // 32))).repeat(32)
    a = np.empty((k // 512, 16))
    for p in range(k // 512):
        a[p, :8] = np.random.permutation(np.resize(levels, 8))
        for g in range(8):
            far = levels[np.abs(levels - a[p, g]) >= 10]
            a[p, g + 8] = far[np.random.randint(len(far))]
    return np.exp2(a.ravel()).repeat(32)


def f64(x):
    return np.asarray(x).astype(np.float64)


def striped(idx):
    return np.tile(np.asarray(idx).reshape(-1, 16).T, (8, 1)).astype(np.uint16)


def unstriped(offs):
    return offs[:16].T.reshape(-1).astype(np.int64)


E2M1 = np.array([0.0, 0.5, 1.0, 1.5, 2.0, 3.0, 4.0, 6.0, -0.0, -0.5, -1.0, -1.5, -2.0, -3.0, -4.0, -6.0])


def pack_weight(w, fmt):
    k, n = w.shape
    w = f64(np.asarray(w, np.float32).astype(ml_dtypes.bfloat16)).reshape(k // 32, 32, n)
    amax = np.abs(w).max(1)
    if fmt == "e4m3":
        byte = np.frexp(amax)[1] - 1 + 127 - 7
    else:
        mant, ex = np.frexp(amax / 6.0)
        byte = np.where(mant > 0.5, ex, ex - 1) + 127
    byte = np.clip(np.where(amax > 0, byte, 1), 1, 254)
    scaled = (w * np.exp2(127.0 - byte)[:, None, :]).reshape(k, n).astype(np.float32)
    by_word = np.ascontiguousarray(scaled.reshape(k // 512, 128, 4, n).transpose(0, 1, 3, 2))
    if fmt == "e4m3":
        words = by_word.astype(ml_dtypes.float8_e4m3fn).view(np.uint8)
    else:
        c = by_word.astype(ml_dtypes.float4_e2m1fn).view(np.uint8) & 0xF
        words = (c[..., 0::2] | (c[..., 1::2] << 4)).reshape(k // 512, 128, 2 * n)
    return np.ascontiguousarray(words), np.ascontiguousarray(byte.astype(np.uint8).reshape(k // 512, 16, n))


def unpack_weight(words, scales, fmt):
    g, _, n = scales.shape
    words = np.ascontiguousarray(words).reshape(g, 128, n, -1)
    if fmt == "e4m3":
        vals = words.view(ml_dtypes.float8_e4m3fn).astype(np.float64)
    else:
        nib = np.empty((g, 128, n, 4), np.uint8)
        nib[..., 0::2] = words & 0xF
        nib[..., 1::2] = words >> 4
        vals = E2M1[nib]
    vals = vals * np.repeat(np.exp2(scales.astype(np.float64) - 127.0), 8, axis=1)[..., None]
    return vals.transpose(0, 1, 3, 2).reshape(g * 512, n)


D, T, I, J, U, Z, E, M = 512, 2048, 512, 256, 1024, 1024, 512, 1024


def setup_inputs():
    n = np.random.standard_normal
    idx = np.random.permutation(T)[:I]
    idx2 = np.random.permutation(U)[:J]
    idx3 = np.random.permutation(Z)[:J]
    idx4 = np.random.permutation(M)[:J]
    fd = mx_kscale(D)
    fi = mx_kscale(I)
    ti = np.ones(T)
    ti[idx] = fi
    keysp = pack_weight(n((D, T)) / fd[:, None], "e4m3")
    return {
        "keys_words": keysp[0],
        "keys_scales": keysp[1],
        "notes": (n((D, U)) * 1.0 / np.sqrt(D) * fd[:, None]).astype(np.float32),
        "users2": (n((D, Z)) * 1.0 / np.sqrt(D) * fd[:, None]).astype(np.float32),
        "rowf": (np.random.uniform(0.02, 0.08, (I, 1)) * fi[:, None]).astype(np.float32),
        "vals": (n((E, T)) / ti).astype(np.float32),
        "held": (n((E, M))).astype(np.float32),
        "hgain": np.tile(np.random.uniform(0.5, 2.0, M), (128, 1)).astype(np.float32),
        "offs": striped(idx),
        "offs2": striped(idx2),
        "offs3": striped(idx3),
        "offs4": striped(idx4),
    }


def reference(keys_words, keys_scales, notes, users2, rowf, vals, held, hgain, offs, offs2, offs3, offs4):
    idx = unstriped(offs)
    idx2 = unstriped(offs2)
    idx3 = unstriped(offs3)
    idx4 = unstriped(offs4)
    keysu = unpack_weight(keys_words, keys_scales, "e4m3")
    keysidxg = keysu[:, idx]
    notesidx2q = mxq(f64(notes)[:, idx2], 0, "e4m3")
    g1 = keysidxg.T @ notesidx2q
    users2idx3q = mxq(f64(users2)[:, idx3], 0, "e4m3")
    g2 = keysidxg.T @ users2idx3q
    g0 = np.maximum(g1, g2)
    gr1 = g0 * f64(rowf)
    vt1 = f64(vals)[:, idx].T
    vt1q = mxq(vt1, 0, "e4m3")
    gr1q = mxq(gr1, 0, "e4m3")
    o = vt1q.T @ gr1q
    y = f64(held)[:, idx4] + o * f64(hgain)[:1][:, idx4]
    return y

@@ -1,0 +1,201 @@
+from contextlib import ExitStack
+
+import concourse.mybir as mybir
+from concourse.masks import make_identity
+
+D, T, I, J, U, E, M = 512, 2048, 512, 256, 1024, 512, 1024
+P = 128
+PACK = 4
+FLOPS = 2 * D * I * J * 2 + 2 * I * E * J
+
+F32 = mybir.dt.float32
+BF16 = mybir.dt.bfloat16
+I32 = mybir.dt.int32
+U32 = mybir.dt.uint32
+U16 = mybir.dt.uint16
+U8 = mybir.dt.uint8
+FP8X4 = mybir.dt.float8_e4m3fn_x4
+COPY = mybir.ActivationFunctionType.Copy
+ALU = mybir.AluOpType
+
+
+def tile_attend_tab_larger_merge_kernel(
+    tc, keys_words, keys_scales, notes, users2, rowf, vals, held, hgain, offs, offs2, offs3, offs4, out
+):
+    nc = tc.nc
+    with ExitStack() as ctx:
+        keep = ctx.enter_context(tc.tile_pool(name="keep", bufs=1))
+        psum = ctx.enter_context(tc.psum_pool(name="psum", bufs=1))
+
+        def sb(name, shape, dtype):
+            return keep.tile(shape, dtype, name=name, align_bytes=64)
+
+        key_bytes = sb("key_bytes", [P, T], U8)
+        nc.vector.memset(key_bytes[:].bitcast(I32), 0)
+        gain_pool = sb("gain_pool", [P, M], F32)
+        nc.vector.memset(gain_pool[:], 0.0)
+        ident = sb("ident", [P, P], F32)
+        make_identity(nc, ident[:])
+
+        def load_pair(name, src, half):
+            tile = sb(name, [P, 2 * U], F32)
+            nc.sync.dma_start(
+                out=tile[:], in_=src.rearrange("(p t) u -> p (t u)", t=PACK)[:, half * 2 * U : (half + 1) * 2 * U]
+            )
+            return tile
+
+        def load_list(name, src):
+            tile = sb(name, list(src.shape), U16)
+            nc.sync.dma_start(out=tile[:], in_=src)
+            return tile
+
+        key_words = sb("key_words", [P, T], U32)
+        nc.sync.dma_start(out=key_words[:].bitcast(I32), in_=keys_words[0].rearrange("p n t -> p (n t)").bitcast(I32))
+        notes_pairs = [load_pair("notes0", notes, 0)]
+        list_i = load_list("list_i", offs)
+        list_notes = load_list("list_notes", offs2)
+        for q in range(4):
+            nc.sync.dma_start(
+                out=key_bytes[32 * q : 32 * q + 4, :].bitcast(I32),
+                in_=keys_scales[0, 4 * q : 4 * q + 4, :].bitcast(I32),
+            )
+        notes_pairs.append(load_pair("notes1", notes, 1))
+        list_users = load_list("list_users", offs3)
+        list_held = load_list("list_held", offs4)
+        users_pairs = [load_pair("users0", users2, 0)]
+        nc.sync.dma_start(out=gain_pool[0:1, :], in_=hgain[0:1, :])
+        row_factor = sb("row_factor", [P, PACK], F32)
+        nc.sync.dma_start(out=row_factor[:], in_=rowf.rearrange("(p t) o -> p (t o)", t=PACK))
+        users_pairs.append(load_pair("users1", users2, 1))
+        vals_tiles = []
+        for k in range(E // P):
+            tile = sb("vals%d" % k, [P, T], F32)
+            nc.sync.dma_start(out=tile[:], in_=vals[k * P : (k + 1) * P, :])
+            vals_tiles.append(tile)
+        held_tiles = []
+        for k in range(E // P):
+            tile = sb("held%d" % k, [P, M], F32)
+            nc.sync.dma_start(out=tile[:], in_=held[k * P : (k + 1) * P, :])
+            held_tiles.append(tile)
+
+        kq = sb("kq", [P, I], U32)
+        ks = sb("ks", [P, I], U8)
+        nc.vector.tensor_copy(out=kq[:].rearrange("p (t s) -> p s t", t=PACK), in_=key_words[:].indirect(list_i[:]))
+        nc.vector.tensor_copy(out=ks[:].rearrange("p (t s) -> p s t", t=PACK), in_=key_bytes[:].indirect(list_i[:]))
+
+        gain_row = sb("gain_row", [P, J], F32)
+        nc.vector.tensor_copy(out=gain_row[:], in_=gain_pool[:].indirect(list_held[:]))
+        gain_cols = psum.tile([P, 2, P], F32, name="gain_cols", tag="turn", bufs=2)
+        for h in range(2):
+            nc.tensor.transpose(gain_cols[:, h, :], gain_row[:, h * P : (h + 1) * P], ident[:])
+        gain_spread = sb("gain_spread", [P, 2, P], F32)
+        nc.vector.tensor_copy(out=gain_spread[:], in_=gain_cols[:, :, 0:1].to_broadcast([P, 2, P]))
+        gain_rows = psum.tile([P, J], F32, name="gain_rows", tag="o", bufs=2)
+        for h in range(2):
+            nc.tensor.transpose(gain_rows[:, h * P : (h + 1) * P], gain_spread[:, h, :], ident[:])
+        gain = sb("gain", [P, J], F32)
+        nc.scalar.copy(out=gain[:], in_=gain_rows[:])
+
+        factor = sb("factor", [P, P, PACK], F32)
+        nc.vector.tensor_copy(out=factor[:], in_=row_factor[:].unsqueeze(1).to_broadcast([P, P, PACK]))
+
+        def scores(name, pairs, lst):
+            planes = sb(name + "_planes", [P, PACK, J], F32)
+            for t in range(PACK):
+                window = pairs[t // 2][:, (t % 2) * U : (t % 2 + 1) * U].indirect(lst[:])
+                if t % 2 == 0:
+                    nc.vector.tensor_copy(out=planes[:, t, :], in_=window)
+                else:
+                    nc.scalar.activation(out=planes[:, t, :], in_=window, func=COPY)
+            woven = sb(name + "_woven", [P, J, PACK], BF16)
+            nc.vector.tensor_copy(out=woven[:], in_=planes[:].rearrange("p t j -> p j t"))
+            codes = sb(name + "_codes", [P, J], U32)
+            scales = sb(name + "_scales", [P, J], U8)
+            nc.vector.quantize_mx(
+                out=codes[:].bitcast(FP8X4), scales=scales[:], in_=woven[:].rearrange("p j t -> p (j t)")
+            )
+            banks = []
+            for h in range(2):
+                bank = psum.tile([P, PACK, P], F32, name="%s_bank%d" % (name, h))
+                for t in range(PACK):
+                    nc.tensor.matmul_mx(
+                        out=bank[:, t, :],
+                        lhsT=kq[:, t * P : (t + 1) * P].bitcast(FP8X4),
+                        lhsT_scale=ks[:, t * P : (t + 1) * P],
+                        rhs=codes[:, h * P : (h + 1) * P].bitcast(FP8X4),
+                        rhs_scale=scales[:, h * P : (h + 1) * P],
+                        start=True,
+                        stop=True,
+                    )
+                banks.append(bank)
+            return banks
+
+        g1_banks = scores("notes", notes_pairs, list_notes)
+        g1 = sb("g1", [P, 2, P, PACK], F32)
+        for h in range(2):
+            nc.scalar.copy(out=g1[:, h], in_=g1_banks[h][:].rearrange("p t j -> p j t"))
+        g2_banks = scores("users", users_pairs, list_users)
+
+        g0 = sb("g0", [P, 2, P, PACK], F32)
+        gr = sb("gr", [P, 2, P, PACK], BF16)
+        for h in range(2):
+            nc.vector.tensor_tensor(
+                out=g0[:, h], in0=g2_banks[h][:].rearrange("p t j -> p j t"), in1=g1[:, h], op=ALU.max
+            )
+        for h in range(2):
+            nc.vector.tensor_tensor(out=gr[:, h], in0=g0[:, h], in1=factor[:], op=ALU.mult)
+        gr_codes = sb("gr_codes", [P, J], U32)
+        gr_scales = sb("gr_scales", [P, J], U8)
+        nc.vector.quantize_mx(
+            out=gr_codes[:].bitcast(FP8X4), scales=gr_scales[:], in_=gr[:].rearrange("p h j t -> p (h j t)")
+        )
+
+        def turn(k):
+            picked = sb("picked%d" % k, [P, I], BF16)
+            nc.scalar.activation(out=picked[:], in_=vals_tiles[k][:].indirect(list_i[:]), func=COPY)
+            words = picked[:].bitcast(F32)
+            turned = psum.tile([P, 2, P], F32, name="turned%d" % k, tag="turn", bufs=2)
+            for u in range(2):
+                nc.tensor.transpose(turned[:, u, :], words[:, u : I // 2 : 2], ident[:])
+            vt = sb("vt%d" % k, [P, P, 2], F32)
+            nc.scalar.copy(out=vt[:], in_=turned[:].rearrange("p u e -> p e u"))
+            return vt
+
+        def product(k, vt):
+            v_codes = sb("v_codes%d" % k, [P, P], U32)
+            v_scales = sb("v_scales%d" % k, [P, P], U8)
+            nc.vector.quantize_mx(
+                out=v_codes[:].bitcast(FP8X4),
+                scales=v_scales[:],
+                in_=vt[:].rearrange("p e u -> p (e u)").bitcast(BF16),
+            )
+            o = psum.tile([P, J], F32, name="o%d" % k, tag="o", bufs=2)
+            nc.tensor.matmul_mx(
+                out=o[:],
+                lhsT=v_codes[:].bitcast(FP8X4),
+                lhsT_scale=v_scales[:],
+                rhs=gr_codes[:].bitcast(FP8X4),
+                rhs_scale=gr_scales[:],
+                start=True,
+                stop=True,
+            )
+            return o
+
+        def gained(k, o):
+            og = sb("og%d" % k, [P, J], F32)
+            nc.vector.tensor_tensor(out=og[:], in0=o[:], in1=gain[:], op=ALU.mult)
+            return og
+
+        def merge(k, og):
+            y = sb("y%d" % k, [P, J], F32)
+            nc.vector.tensor_tensor(out=y[:], in0=held_tiles[k][:].indirect(list_held[:]), in1=og[:], op=ALU.add)
+            nc.sync.dma_start(out=out[k * P : (k + 1) * P, :], in_=y[:])
+
+        vts = [turn(k) for k in range(4)]
+        ogs = [gained(k, product(k, vts[k])) for k in range(3)]
+        merge(0, ogs[0])
+        last = product(3, vts[3])
+        merge(1, ogs[1])
+        ogs.append(gained(3, last))
+        merge(2, ogs[2])
+        merge(3, ogs[3])

@@ -26,13 +26,17 @@ def tile_attend_tab_larger_merge_kernel(
     with ExitStack() as ctx:
         keep = ctx.enter_context(tc.tile_pool(name="keep", bufs=1))
         psum = ctx.enter_context(tc.psum_pool(name="psum", bufs=1))
+        shared = ctx.enter_context(tc.tile_pool(name="shared", bufs=1))
+
+        def placed(name, shape, dtype, kib):
+            return shared.tile(shape, dtype, name=name, align_bytes=64, offset=512 * kib)
 
         def sb(name, shape, dtype):
             return keep.tile(shape, dtype, name=name, align_bytes=64)
 
-        key_bytes = sb("key_bytes", [P, T], U8)
-        nc.vector.memset(key_bytes[:].bitcast(I32), 0)
-        gain_pool = sb("gain_pool", [P, M], F32)
+        key_bytes = placed("key_bytes", [P, T], U8, 0)
+        nc.gpsimd.memset(key_bytes[:].bitcast(I32), 0)
+        gain_pool = placed("gain_pool", [P, M], F32, 4)
         nc.vector.memset(gain_pool[:], 0.0)
         ident = sb("ident", [P, P], F32)
         make_identity(nc, ident[:])
@@ -51,22 +55,21 @@ def tile_attend_tab_larger_merge_kernel(
 
         key_words = sb("key_words", [P, T], U32)
         nc.sync.dma_start(out=key_words[:].bitcast(I32), in_=keys_words[0].rearrange("p n t -> p (n t)").bitcast(I32))
-        notes_pairs = [load_pair("notes0", notes, 0)]
         list_i = load_list("list_i", offs)
         list_notes = load_list("list_notes", offs2)
+        list_users = load_list("list_users", offs3)
+        list_held = load_list("list_held", offs4)
+        row_factor = sb("row_factor", [P, PACK], F32)
+        nc.sync.dma_start(out=row_factor[:], in_=rowf.rearrange("(p t) o -> p (t o)", t=PACK))
+        notes_pairs = [load_pair("notes0", notes, 0)]
         for q in range(4):
             nc.sync.dma_start(
                 out=key_bytes[32 * q : 32 * q + 4, :].bitcast(I32),
                 in_=keys_scales[0, 4 * q : 4 * q + 4, :].bitcast(I32),
             )
-        notes_pairs.append(load_pair("notes1", notes, 1))
-        list_users = load_list("list_users", offs3)
-        list_held = load_list("list_held", offs4)
-        users_pairs = [load_pair("users0", users2, 0)]
         nc.sync.dma_start(out=gain_pool[0:1, :], in_=hgain[0:1, :])
-        row_factor = sb("row_factor", [P, PACK], F32)
-        nc.sync.dma_start(out=row_factor[:], in_=rowf.rearrange("(p t) o -> p (t o)", t=PACK))
-        users_pairs.append(load_pair("users1", users2, 1))
+        notes_pairs.append(load_pair("notes1", notes, 1))
+        users_pairs = [load_pair("users%d" % h, users2, h) for h in range(2)]
         vals_tiles = []
         for k in range(E // P):
             tile = sb("vals%d" % k, [P, T], F32)
@@ -78,45 +81,27 @@ def tile_attend_tab_larger_merge_kernel(
             nc.sync.dma_start(out=tile[:], in_=held[k * P : (k + 1) * P, :])
             held_tiles.append(tile)
 
-        kq = sb("kq", [P, I], U32)
-        ks = sb("ks", [P, I], U8)
-        nc.vector.tensor_copy(out=kq[:].rearrange("p (t s) -> p s t", t=PACK), in_=key_words[:].indirect(list_i[:]))
-        nc.vector.tensor_copy(out=ks[:].rearrange("p (t s) -> p s t", t=PACK), in_=key_bytes[:].indirect(list_i[:]))
-
-        gain_row = sb("gain_row", [P, J], F32)
-        nc.vector.tensor_copy(out=gain_row[:], in_=gain_pool[:].indirect(list_held[:]))
-        gain_cols = psum.tile([P, 2, P], F32, name="gain_cols", tag="turn", bufs=2)
-        for h in range(2):
-            nc.tensor.transpose(gain_cols[:, h, :], gain_row[:, h * P : (h + 1) * P], ident[:])
-        gain_spread = sb("gain_spread", [P, 2, P], F32)
-        nc.vector.tensor_copy(out=gain_spread[:], in_=gain_cols[:, :, 0:1].to_broadcast([P, 2, P]))
-        gain_rows = psum.tile([P, J], F32, name="gain_rows", tag="o", bufs=2)
-        for h in range(2):
-            nc.tensor.transpose(gain_rows[:, h * P : (h + 1) * P], gain_spread[:, h, :], ident[:])
-        gain = sb("gain", [P, J], F32)
-        nc.scalar.copy(out=gain[:], in_=gain_rows[:])
-
-        factor = sb("factor", [P, P, PACK], F32)
-        nc.vector.tensor_copy(out=factor[:], in_=row_factor[:].unsqueeze(1).to_broadcast([P, P, PACK]))
-
-        def scores(name, pairs, lst):
-            planes = sb(name + "_planes", [P, PACK, J], F32)
+        def quantised_columns(name, pairs, lst, place):
+            planes = placed(name + "_planes", [P, PACK, J], F32, place)
             for t in range(PACK):
                 window = pairs[t // 2][:, (t % 2) * U : (t % 2 + 1) * U].indirect(lst[:])
                 if t % 2 == 0:
                     nc.vector.tensor_copy(out=planes[:, t, :], in_=window)
                 else:
                     nc.scalar.activation(out=planes[:, t, :], in_=window, func=COPY)
-            woven = sb(name + "_woven", [P, J, PACK], BF16)
+            woven = placed(name + "_woven", [P, J, PACK], BF16, 20)
             nc.vector.tensor_copy(out=woven[:], in_=planes[:].rearrange("p t j -> p j t"))
             codes = sb(name + "_codes", [P, J], U32)
             scales = sb(name + "_scales", [P, J], U8)
             nc.vector.quantize_mx(
                 out=codes[:].bitcast(FP8X4), scales=scales[:], in_=woven[:].rearrange("p j t -> p (j t)")
             )
+            return codes, scales
+
+        def table(name, codes, scales):
             banks = []
             for h in range(2):
-                bank = psum.tile([P, PACK, P], F32, name="%s_bank%d" % (name, h))
+                bank = psum.tile([P, PACK, P], F32, name="%s_bank%d" % (name, h), tag=name, bufs=2)
                 for t in range(PACK):
                     nc.tensor.matmul_mx(
                         out=bank[:, t, :],
@@ -130,72 +115,105 @@ def tile_attend_tab_larger_merge_kernel(
                 banks.append(bank)
             return banks
 
-        g1_banks = scores("notes", notes_pairs, list_notes)
-        g1 = sb("g1", [P, 2, P, PACK], F32)
+        kq = sb("kq", [P, I], U32)
+        ks = sb("ks", [P, I], U8)
+        nc.vector.tensor_copy(out=kq[:].rearrange("p (t s) -> p s t", t=PACK), in_=key_words[:].indirect(list_i[:]))
+        factor = sb("factor", [P, P, PACK], F32)
+        nc.vector.tensor_copy(out=factor[:], in_=row_factor[:].unsqueeze(1).to_broadcast([P, P, PACK]))
+        nc.vector.tensor_copy(out=ks[:].rearrange("p (t s) -> p s t", t=PACK), in_=key_bytes[:].indirect(list_i[:]))
+        notes_mx = quantised_columns("notes", notes_pairs, list_notes, 12)
+
+        gain_row = sb("gain_row", [P, J], F32)
+        nc.scalar.activation(out=gain_row[:], in_=gain_pool[:].indirect(list_held[:]), func=COPY)
+        gain_cols = psum.tile([P, 2, P], F32, name="gain_cols")
         for h in range(2):
-            nc.scalar.copy(out=g1[:, h], in_=g1_banks[h][:].rearrange("p t j -> p j t"))
-        g2_banks = scores("users", users_pairs, list_users)
+            nc.tensor.transpose(gain_cols[:, h, :], gain_row[:, h * P : (h + 1) * P], ident[:])
+        gain_spread = sb("gain_spread", [P, 2, P], F32)
+        nc.vector.tensor_copy(out=gain_spread[:], in_=gain_cols[:, :, 0:1].to_broadcast([P, 2, P]))
+        g1_banks = table("notes", *notes_mx)
+        gain_rows = psum.tile([P, J], F32, name="gain_rows")
+        for h in range(2):
+            nc.tensor.transpose(gain_rows[:, h * P : (h + 1) * P], gain_spread[:, h, :], ident[:])
+
+        users_mx = quantised_columns("users", users_pairs, list_users, 0)
+        gain = placed("gain", [P, J], F32, 4)
+        nc.scalar.copy(out=gain[:], in_=gain_rows[:])
+        g2_banks = table("users", *users_mx)
+        g1 = placed("g1", [P, 2, P, PACK], F32, 20)
+        for h in range(2):
+            nc.vector.tensor_copy(out=g1[:, h], in_=g1_banks[h][:].rearrange("p t j -> p j t"))
 
         g0 = sb("g0", [P, 2, P, PACK], F32)
-        gr = sb("gr", [P, 2, P, PACK], BF16)
+        gr = [placed("gr%d" % h, [P, P, PACK], BF16, 28 + 2 * h) for h in range(2)]
         for h in range(2):
             nc.vector.tensor_tensor(
                 out=g0[:, h], in0=g2_banks[h][:].rearrange("p t j -> p j t"), in1=g1[:, h], op=ALU.max
             )
         for h in range(2):
-            nc.vector.tensor_tensor(out=gr[:, h], in0=g0[:, h], in1=factor[:], op=ALU.mult)
+            nc.vector.tensor_tensor(out=gr[h][:], in0=g0[:, h], in1=factor[:], op=ALU.mult)
         gr_codes = sb("gr_codes", [P, J], U32)
         gr_scales = sb("gr_scales", [P, J], U8)
-        nc.vector.quantize_mx(
-            out=gr_codes[:].bitcast(FP8X4), scales=gr_scales[:], in_=gr[:].rearrange("p h j t -> p (h j t)")
-        )
+        for h in range(2):
+            nc.vector.quantize_mx(
+                out=gr_codes[:, h * P : (h + 1) * P].bitcast(FP8X4),
+                scales=gr_scales[:, h * P : (h + 1) * P],
+                in_=gr[h][:].rearrange("p j t -> p (j t)"),
+            )
 
-        def turn(k):
-            picked = sb("picked%d" % k, [P, I], BF16)
-            nc.scalar.activation(out=picked[:], in_=vals_tiles[k][:].indirect(list_i[:]), func=COPY)
-            words = picked[:].bitcast(F32)
-            turned = psum.tile([P, 2, P], F32, name="turned%d" % k, tag="turn", bufs=2)
-            for u in range(2):
-                nc.tensor.transpose(turned[:, u, :], words[:, u : I // 2 : 2], ident[:])
-            vt = sb("vt%d" % k, [P, P, 2], F32)
-            nc.scalar.copy(out=vt[:], in_=turned[:].rearrange("p u e -> p e u"))
-            return vt
+        def turn(ks_, vt, copy):
+            n = len(ks_)
+            turned = psum.tile([P, n, 2, P], F32, name="turned%d" % ks_[0], tag="users", bufs=2)
+            for a, k in enumerate(ks_):
+                picked = placed("picked%d" % k, [P, I], BF16, (0, 2, 6, 6)[k])
+                nc.scalar.activation(out=picked[:], in_=vals_tiles[k][:].indirect(list_i[:]), func=COPY)
+                words = picked[:].bitcast(F32)
+                for u in range(2):
+                    nc.tensor.transpose(turned[:, a, u, :], words[:, u : I // 2 : 2], ident[:])
+            copy(out=vt[:], in_=turned[:].rearrange("p a u e -> p a e u"))
 
-        def product(k, vt):
-            v_codes = sb("v_codes%d" % k, [P, P], U32)
-            v_scales = sb("v_scales%d" % k, [P, P], U8)
+        def product(name, n, vt, v_codes):
+            v_scales = sb("v_scales" + name, [P, n * P], U8)
             nc.vector.quantize_mx(
                 out=v_codes[:].bitcast(FP8X4),
                 scales=v_scales[:],
-                in_=vt[:].rearrange("p e u -> p (e u)").bitcast(BF16),
+                in_=vt[:].rearrange("p a e u -> p (a e u)").bitcast(BF16),
             )
-            o = psum.tile([P, J], F32, name="o%d" % k, tag="o", bufs=2)
-            nc.tensor.matmul_mx(
-                out=o[:],
-                lhsT=v_codes[:].bitcast(FP8X4),
-                lhsT_scale=v_scales[:],
-                rhs=gr_codes[:].bitcast(FP8X4),
-                rhs_scale=gr_scales[:],
-                start=True,
-                stop=True,
-            )
+            o = psum.tile([P, n, J], F32, name="o" + name, tag="notes", bufs=2)
+            for a in range(n):
+                nc.tensor.matmul_mx(
+                    out=o[:, a, :],
+                    lhsT=v_codes[:, a * P : (a + 1) * P].bitcast(FP8X4),
+                    lhsT_scale=v_scales[:, a * P : (a + 1) * P],
+                    rhs=gr_codes[:].bitcast(FP8X4),
+                    rhs_scale=gr_scales[:],
+                    start=True,
+                    stop=True,
+                )
             return o
 
-        def gained(k, o):
-            og = sb("og%d" % k, [P, J], F32)
-            nc.vector.tensor_tensor(out=og[:], in0=o[:], in1=gain[:], op=ALU.mult)
-            return og
+        def gained(o, og, n):
+            nc.vector.tensor_tensor(
+                out=og[:], in0=o[:], in1=gain[:].unsqueeze(1).to_broadcast([P, n, J]), op=ALU.mult
+            )
 
-        def merge(k, og):
-            y = sb("y%d" % k, [P, J], F32)
-            nc.vector.tensor_tensor(out=y[:], in0=held_tiles[k][:].indirect(list_held[:]), in1=og[:], op=ALU.add)
+        def merge(k, og, y):
+            nc.vector.tensor_tensor(out=y[:], in0=held_tiles[k][:].indirect(list_held[:]), in1=og, op=ALU.add)
             nc.sync.dma_start(out=out[k * P : (k + 1) * P, :], in_=y[:])
 
-        vts = [turn(k) for k in range(4)]
-        ogs = [gained(k, product(k, vts[k])) for k in range(3)]
-        merge(0, ogs[0])
-        last = product(3, vts[3])
-        merge(1, ogs[1])
-        ogs.append(gained(3, last))
-        merge(2, ogs[2])
-        merge(3, ogs[3])
+        vt01 = placed("vt01", [P, 2, P, 2], F32, 28)
+        turn((0, 1), vt01, nc.vector.tensor_copy)
+        og01 = placed("og01", [P, 2, J], F32, 36)
+        gained(product("01", 2, vt01, sb("v_codes01", [P, 2 * P], U32)), og01, 2)
+        vt2 = placed("vt2", [P, 1, P, 2], F32, 33)
+        turn((2,), vt2, nc.scalar.copy)
+        og2 = sb("og2", [P, 1, J], F32)
+        gained(product("2", 1, vt2, sb("v_codes2", [P, P], U32)), og2, 1)
+        vt3 = placed("vt3", [P, 1, P, 2], F32, 40)
+        turn((3,), vt3, nc.scalar.copy)
+        merge(0, og01[:, 0, :], placed("y0", [P, J], F32, 32))
+        merge(1, og01[:, 1, :], placed("y1", [P, J], F32, 34))
+        o3 = product("3", 1, vt3, placed("v_codes3", [P, P], U32, 38))
+        merge(2, og2[:, 0, :], placed("y2", [P, J], F32, 40))
+        og3 = sb("og3", [P, 1, J], F32)
+        gained(o3, og3, 1)
+        merge(3, og3[:, 0, :], sb("y3", [P, J], F32))

@@ -26,17 +26,13 @@ def tile_attend_tab_larger_merge_kernel(
     with ExitStack() as ctx:
         keep = ctx.enter_context(tc.tile_pool(name="keep", bufs=1))
         psum = ctx.enter_context(tc.psum_pool(name="psum", bufs=1))
-        shared = ctx.enter_context(tc.tile_pool(name="shared", bufs=1))
 
-        def placed(name, shape, dtype, kib):
-            return shared.tile(shape, dtype, name=name, align_bytes=64, offset=512 * kib)
+        def sb(name, shape, dtype, tag=None):
+            return keep.tile(shape, dtype, name=name, tag=tag or name, align_bytes=64)
 
-        def sb(name, shape, dtype):
-            return keep.tile(shape, dtype, name=name, align_bytes=64)
-
-        key_bytes = placed("key_bytes", [P, T], U8, 0)
+        key_bytes = sb("key_bytes", [P, T], U8)
         nc.gpsimd.memset(key_bytes[:].bitcast(I32), 0)
-        gain_pool = placed("gain_pool", [P, M], F32, 4)
+        gain_pool = sb("gain_pool", [P, M], F32)
         nc.vector.memset(gain_pool[:], 0.0)
         ident = sb("ident", [P, P], F32)
         make_identity(nc, ident[:])
@@ -56,20 +52,20 @@ def tile_attend_tab_larger_merge_kernel(
         key_words = sb("key_words", [P, T], U32)
         nc.sync.dma_start(out=key_words[:].bitcast(I32), in_=keys_words[0].rearrange("p n t -> p (n t)").bitcast(I32))
         list_i = load_list("list_i", offs)
-        list_notes = load_list("list_notes", offs2)
-        list_users = load_list("list_users", offs3)
-        list_held = load_list("list_held", offs4)
-        row_factor = sb("row_factor", [P, PACK], F32)
-        nc.sync.dma_start(out=row_factor[:], in_=rowf.rearrange("(p t) o -> p (t o)", t=PACK))
-        notes_pairs = [load_pair("notes0", notes, 0)]
         for q in range(4):
             nc.sync.dma_start(
                 out=key_bytes[32 * q : 32 * q + 4, :].bitcast(I32),
                 in_=keys_scales[0, 4 * q : 4 * q + 4, :].bitcast(I32),
             )
+        list_notes = load_list("list_notes", offs2)
+        notes_pairs = [load_pair("notes%d" % h, notes, h) for h in range(2)]
+        list_held = load_list("list_held", offs4)
         nc.sync.dma_start(out=gain_pool[0:1, :], in_=hgain[0:1, :])
-        notes_pairs.append(load_pair("notes1", notes, 1))
-        users_pairs = [load_pair("users%d" % h, users2, h) for h in range(2)]
+        row_factor = sb("row_factor", [P, PACK], F32)
+        nc.sync.dma_start(out=row_factor[:], in_=rowf.rearrange("(p t) o -> p (t o)", t=PACK))
+        users_pairs = [load_pair("users0", users2, 0)]
+        list_users = load_list("list_users", offs3)
+        users_pairs.append(load_pair("users1", users2, 1))
         vals_tiles = []
         for k in range(E // P):
             tile = sb("vals%d" % k, [P, T], F32)
@@ -81,21 +77,27 @@ def tile_attend_tab_larger_merge_kernel(
             nc.sync.dma_start(out=tile[:], in_=held[k * P : (k + 1) * P, :])
             held_tiles.append(tile)
 
-        def quantised_columns(name, pairs, lst, place):
-            planes = placed(name + "_planes", [P, PACK, J], F32, place)
+        def quantised_columns(name, pairs, lst, on_scalar):
+            planes = sb(name + "_planes", [P, PACK, J], F32)
             for t in range(PACK):
                 window = pairs[t // 2][:, (t % 2) * U : (t % 2 + 1) * U].indirect(lst[:])
-                if t % 2 == 0:
+                if t not in on_scalar:
                     nc.vector.tensor_copy(out=planes[:, t, :], in_=window)
                 else:
                     nc.scalar.activation(out=planes[:, t, :], in_=window, func=COPY)
-            woven = placed(name + "_woven", [P, J, PACK], BF16, 20)
-            nc.vector.tensor_copy(out=woven[:], in_=planes[:].rearrange("p t j -> p j t"))
+            woven = sb(name + "_woven", [P, J, PACK], BF16)
+            for h in range(2):
+                cols = slice(h * P, (h + 1) * P)
+                nc.vector.tensor_copy(out=woven[:, cols, :], in_=planes[:, :, cols].rearrange("p t j -> p j t"))
             codes = sb(name + "_codes", [P, J], U32)
             scales = sb(name + "_scales", [P, J], U8)
-            nc.vector.quantize_mx(
-                out=codes[:].bitcast(FP8X4), scales=scales[:], in_=woven[:].rearrange("p j t -> p (j t)")
-            )
+            for h in range(2):
+                cols = slice(h * P, (h + 1) * P)
+                nc.vector.quantize_mx(
+                    out=codes[:, cols].bitcast(FP8X4),
+                    scales=scales[:, cols],
+                    in_=woven[:, cols, :].rearrange("p j t -> p (j t)"),
+                )
             return codes, scales
 
         def table(name, codes, scales):
@@ -118,10 +120,10 @@ def tile_attend_tab_larger_merge_kernel(
         kq = sb("kq", [P, I], U32)
         ks = sb("ks", [P, I], U8)
         nc.vector.tensor_copy(out=kq[:].rearrange("p (t s) -> p s t", t=PACK), in_=key_words[:].indirect(list_i[:]))
+        nc.vector.tensor_copy(out=ks[:].rearrange("p (t s) -> p s t", t=PACK), in_=key_bytes[:].indirect(list_i[:]))
+        notes_mx = quantised_columns("notes", notes_pairs, list_notes, (1, 3))
         factor = sb("factor", [P, P, PACK], F32)
         nc.vector.tensor_copy(out=factor[:], in_=row_factor[:].unsqueeze(1).to_broadcast([P, P, PACK]))
-        nc.vector.tensor_copy(out=ks[:].rearrange("p (t s) -> p s t", t=PACK), in_=key_bytes[:].indirect(list_i[:]))
-        notes_mx = quantised_columns("notes", notes_pairs, list_notes, 12)
 
         gain_row = sb("gain_row", [P, J], F32)
         nc.scalar.activation(out=gain_row[:], in_=gain_pool[:].indirect(list_held[:]), func=COPY)
@@ -129,22 +131,22 @@ def tile_attend_tab_larger_merge_kernel(
         for h in range(2):
             nc.tensor.transpose(gain_cols[:, h, :], gain_row[:, h * P : (h + 1) * P], ident[:])
         gain_spread = sb("gain_spread", [P, 2, P], F32)
-        nc.vector.tensor_copy(out=gain_spread[:], in_=gain_cols[:, :, 0:1].to_broadcast([P, 2, P]))
+        nc.scalar.copy(out=gain_spread[:], in_=gain_cols[:, :, 0:1].to_broadcast([P, 2, P]))
         g1_banks = table("notes", *notes_mx)
         gain_rows = psum.tile([P, J], F32, name="gain_rows")
         for h in range(2):
             nc.tensor.transpose(gain_rows[:, h * P : (h + 1) * P], gain_spread[:, h, :], ident[:])
-
-        users_mx = quantised_columns("users", users_pairs, list_users, 0)
-        gain = placed("gain", [P, J], F32, 4)
+        gain = sb("gain", [P, J], F32)
         nc.scalar.copy(out=gain[:], in_=gain_rows[:])
-        g2_banks = table("users", *users_mx)
-        g1 = placed("g1", [P, 2, P, PACK], F32, 20)
+
+        g1 = sb("g1", [P, 2, P, PACK], F32)
         for h in range(2):
             nc.vector.tensor_copy(out=g1[:, h], in_=g1_banks[h][:].rearrange("p t j -> p j t"))
+        users_mx = quantised_columns("users", users_pairs, list_users, (1, 3))
+        g2_banks = table("users", *users_mx)
 
         g0 = sb("g0", [P, 2, P, PACK], F32)
-        gr = [placed("gr%d" % h, [P, P, PACK], BF16, 28 + 2 * h) for h in range(2)]
+        gr = [sb("gr%d" % h, [P, P, PACK], BF16) for h in range(2)]
         for h in range(2):
             nc.vector.tensor_tensor(
                 out=g0[:, h], in0=g2_banks[h][:].rearrange("p t j -> p j t"), in1=g1[:, h], op=ALU.max
@@ -164,7 +166,7 @@ def tile_attend_tab_larger_merge_kernel(
             n = len(ks_)
             turned = psum.tile([P, n, 2, P], F32, name="turned%d" % ks_[0], tag="users", bufs=2)
             for a, k in enumerate(ks_):
-                picked = placed("picked%d" % k, [P, I], BF16, (0, 2, 6, 6)[k])
+                picked = sb("picked%d" % k, [P, I], BF16)
                 nc.scalar.activation(out=picked[:], in_=vals_tiles[k][:].indirect(list_i[:]), func=COPY)
                 words = picked[:].bitcast(F32)
                 for u in range(2):
@@ -200,20 +202,20 @@ def tile_attend_tab_larger_merge_kernel(
             nc.vector.tensor_tensor(out=y[:], in0=held_tiles[k][:].indirect(list_held[:]), in1=og, op=ALU.add)
             nc.sync.dma_start(out=out[k * P : (k + 1) * P, :], in_=y[:])
 
-        vt01 = placed("vt01", [P, 2, P, 2], F32, 28)
+        vt01 = sb("vt01", [P, 2, P, 2], F32)
         turn((0, 1), vt01, nc.vector.tensor_copy)
-        og01 = placed("og01", [P, 2, J], F32, 36)
+        og01 = sb("og01", [P, 2, J], F32)
         gained(product("01", 2, vt01, sb("v_codes01", [P, 2 * P], U32)), og01, 2)
-        vt2 = placed("vt2", [P, 1, P, 2], F32, 33)
+        vt2 = sb("vt2", [P, 1, P, 2], F32)
         turn((2,), vt2, nc.scalar.copy)
         og2 = sb("og2", [P, 1, J], F32)
         gained(product("2", 1, vt2, sb("v_codes2", [P, P], U32)), og2, 1)
-        vt3 = placed("vt3", [P, 1, P, 2], F32, 40)
+        vt3 = sb("vt3", [P, 1, P, 2], F32)
         turn((3,), vt3, nc.scalar.copy)
-        merge(0, og01[:, 0, :], placed("y0", [P, J], F32, 32))
-        merge(1, og01[:, 1, :], placed("y1", [P, J], F32, 34))
-        o3 = product("3", 1, vt3, placed("v_codes3", [P, P], U32, 38))
-        merge(2, og2[:, 0, :], placed("y2", [P, J], F32, 40))
-        og3 = sb("og3", [P, 1, J], F32)
+        merge(0, og01[:, 0, :], sb("y0", [P, J], F32))
+        merge(1, og01[:, 1, :], sb("y1", [P, J], F32))
+        o3 = product("3", 1, vt3, sb("v_codes3", [P, P], U32, tag="og01"))
+        merge(2, og2[:, 0, :], sb("y2", [P, J], F32))
+        og3 = sb("og3", [P, 1, J], F32, tag="og2")
         gained(o3, og3, 1)
         merge(3, og3[:, 0, :], sb("y3", [P, J], F32))

@@ -37,9 +37,9 @@ def tile_attend_tab_larger_merge_kernel(
         ident = sb("ident", [P, P], F32)
         make_identity(nc, ident[:])
 
-        def load_pair(name, src, half):
+        def load_pair(queue, name, src, half):
             tile = sb(name, [P, 2 * U], F32)
-            nc.sync.dma_start(
+            queue.dma_start(
                 out=tile[:], in_=src.rearrange("(p t) u -> p (t u)", t=PACK)[:, half * 2 * U : (half + 1) * 2 * U]
             )
             return tile
@@ -50,22 +50,23 @@ def tile_attend_tab_larger_merge_kernel(
             return tile
 
         key_words = sb("key_words", [P, T], U32)
-        nc.sync.dma_start(out=key_words[:].bitcast(I32), in_=keys_words[0].rearrange("p n t -> p (n t)").bitcast(I32))
+        nc.scalar.dma_start(
+            out=key_words[:].bitcast(I32), in_=keys_words[0].rearrange("p n t -> p (n t)").bitcast(I32)
+        )
+        notes_pairs = [load_pair(nc.scalar, "notes%d" % h, notes, h) for h in range(2)]
         list_i = load_list("list_i", offs)
+        list_held = load_list("list_held", offs4)
+        nc.sync.dma_start(out=gain_pool[0:1, :], in_=hgain[0:1, :])
         for q in range(4):
             nc.sync.dma_start(
                 out=key_bytes[32 * q : 32 * q + 4, :].bitcast(I32),
                 in_=keys_scales[0, 4 * q : 4 * q + 4, :].bitcast(I32),
             )
         list_notes = load_list("list_notes", offs2)
-        notes_pairs = [load_pair("notes%d" % h, notes, h) for h in range(2)]
-        list_held = load_list("list_held", offs4)
-        nc.sync.dma_start(out=gain_pool[0:1, :], in_=hgain[0:1, :])
         row_factor = sb("row_factor", [P, PACK], F32)
         nc.sync.dma_start(out=row_factor[:], in_=rowf.rearrange("(p t) o -> p (t o)", t=PACK))
-        users_pairs = [load_pair("users0", users2, 0)]
         list_users = load_list("list_users", offs3)
-        users_pairs.append(load_pair("users1", users2, 1))
+        users_pairs = [load_pair(nc.sync, "users%d" % h, users2, h) for h in range(2)]
         vals_tiles = []
         for k in range(E // P):
             tile = sb("vals%d" % k, [P, T], F32)
@@ -117,6 +118,19 @@ def tile_attend_tab_larger_merge_kernel(
                 banks.append(bank)
             return banks
 
+        gain_row = sb("gain_row", [P, J], F32)
+        nc.scalar.activation(out=gain_row[:], in_=gain_pool[:].indirect(list_held[:]), func=COPY)
+        gain_cols = psum.tile([P, 2, P], F32, name="gain_cols")
+        for h in range(2):
+            nc.tensor.transpose(gain_cols[:, h, :], gain_row[:, h * P : (h + 1) * P], ident[:])
+        gain_spread = sb("gain_spread", [P, 2, P], F32)
+        nc.scalar.copy(out=gain_spread[:], in_=gain_cols[:, :, 0:1].to_broadcast([P, 2, P]))
+        gain_rows = psum.tile([P, J], F32, name="gain_rows")
+        for h in range(2):
+            nc.tensor.transpose(gain_rows[:, h * P : (h + 1) * P], gain_spread[:, h, :], ident[:])
+        gain = sb("gain", [P, J], F32)
+        nc.scalar.copy(out=gain[:], in_=gain_rows[:])
+
         kq = sb("kq", [P, I], U32)
         ks = sb("ks", [P, I], U8)
         nc.vector.tensor_copy(out=kq[:].rearrange("p (t s) -> p s t", t=PACK), in_=key_words[:].indirect(list_i[:]))
@@ -125,20 +139,7 @@ def tile_attend_tab_larger_merge_kernel(
         factor = sb("factor", [P, P, PACK], F32)
         nc.vector.tensor_copy(out=factor[:], in_=row_factor[:].unsqueeze(1).to_broadcast([P, P, PACK]))
 
-        gain_row = sb("gain_row", [P, J], F32)
-        nc.scalar.activation(out=gain_row[:], in_=gain_pool[:].indirect(list_held[:]), func=COPY)
-        gain_cols = psum.tile([P, 2, P], F32, name="gain_cols")
-        for h in range(2):
-            nc.tensor.transpose(gain_cols[:, h, :], gain_row[:, h * P : (h + 1) * P], ident[:])
-        gain_spread = sb("gain_spread", [P, 2, P], F32)
-        nc.scalar.copy(out=gain_spread[:], in_=gain_cols[:, :, 0:1].to_broadcast([P, 2, P]))
         g1_banks = table("notes", *notes_mx)
-        gain_rows = psum.tile([P, J], F32, name="gain_rows")
-        for h in range(2):
-            nc.tensor.transpose(gain_rows[:, h * P : (h + 1) * P], gain_spread[:, h, :], ident[:])
-        gain = sb("gain", [P, J], F32)
-        nc.scalar.copy(out=gain[:], in_=gain_rows[:])
-
         g1 = sb("g1", [P, 2, P, PACK], F32)
         for h in range(2):
             nc.vector.tensor_copy(out=g1[:, h], in_=g1_banks[h][:].rearrange("p t j -> p j t"))
@@ -162,60 +163,62 @@ def tile_attend_tab_larger_merge_kernel(
                 in_=gr[h][:].rearrange("p j t -> p (j t)"),
             )
 
-        def turn(ks_, vt, copy):
-            n = len(ks_)
-            turned = psum.tile([P, n, 2, P], F32, name="turned%d" % ks_[0], tag="users", bufs=2)
-            for a, k in enumerate(ks_):
+        def turn(tiles, vt):
+            turned = psum.tile([P, len(tiles), 2, P], F32, name="turned%d" % tiles[0], tag="users", bufs=2)
+            for a, k in enumerate(tiles):
                 picked = sb("picked%d" % k, [P, I], BF16)
                 nc.scalar.activation(out=picked[:], in_=vals_tiles[k][:].indirect(list_i[:]), func=COPY)
                 words = picked[:].bitcast(F32)
                 for u in range(2):
                     nc.tensor.transpose(turned[:, a, u, :], words[:, u : I // 2 : 2], ident[:])
-            copy(out=vt[:], in_=turned[:].rearrange("p a u e -> p a e u"))
+            nc.vector.tensor_copy(out=vt, in_=turned[:].rearrange("p a u e -> p a e u"))
 
-        def product(name, n, vt, v_codes):
-            v_scales = sb("v_scales" + name, [P, n * P], U8)
+        def gained_products(banks):
+            first = banks[0][0]
+            n = sum(len(tiles) for tiles in banks)
+            vt = sb("vt%d" % first, [P, n, P, 2], F32)
+            for tiles in banks:
+                turn(tiles, vt[:, tiles[0] - first : tiles[-1] + 1 - first])
+            v_codes = sb("v_codes%d" % first, [P, n * P], U32)
+            v_scales = sb("v_scales%d" % first, [P, n * P], U8)
             nc.vector.quantize_mx(
                 out=v_codes[:].bitcast(FP8X4),
                 scales=v_scales[:],
                 in_=vt[:].rearrange("p a e u -> p (a e u)").bitcast(BF16),
             )
-            o = psum.tile([P, n, J], F32, name="o" + name, tag="notes", bufs=2)
-            for a in range(n):
-                nc.tensor.matmul_mx(
-                    out=o[:, a, :],
-                    lhsT=v_codes[:, a * P : (a + 1) * P].bitcast(FP8X4),
-                    lhsT_scale=v_scales[:, a * P : (a + 1) * P],
-                    rhs=gr_codes[:].bitcast(FP8X4),
-                    rhs_scale=gr_scales[:],
-                    start=True,
-                    stop=True,
+            gained = []
+            for tiles in banks:
+                o = psum.tile([P, len(tiles), J], F32, name="o%d" % tiles[0], tag="notes", bufs=2)
+                for a, k in enumerate(tiles):
+                    cols = slice((k - first) * P, (k - first + 1) * P)
+                    nc.tensor.matmul_mx(
+                        out=o[:, a, :],
+                        lhsT=v_codes[:, cols].bitcast(FP8X4),
+                        lhsT_scale=v_scales[:, cols],
+                        rhs=gr_codes[:].bitcast(FP8X4),
+                        rhs_scale=gr_scales[:],
+                        start=True,
+                        stop=True,
+                    )
+                og = sb("og%d" % tiles[0], [P, len(tiles), J], F32)
+                nc.vector.tensor_tensor(
+                    out=og[:], in0=o[:], in1=gain[:].unsqueeze(1).to_broadcast([P, len(tiles), J]), op=ALU.mult
                 )
-            return o
+                gained.extend(og[:, a, :] for a in range(len(tiles)))
+            return gained
 
-        def gained(o, og, n):
-            nc.vector.tensor_tensor(
-                out=og[:], in0=o[:], in1=gain[:].unsqueeze(1).to_broadcast([P, n, J]), op=ALU.mult
-            )
-
-        def merge(k, og, y):
-            nc.vector.tensor_tensor(out=y[:], in0=held_tiles[k][:].indirect(list_held[:]), in1=og, op=ALU.add)
+        def merge(k, og, fused):
+            y = sb("y%d" % k, [P, J], F32)
+            picked_held = sb("picked_held%d" % k, [P, J - fused], F32)
+            window = held_tiles[k][:]
+            nc.scalar.activation(out=picked_held[:], in_=window.indirect(list_held[:, fused // 16 :]), func=COPY)
+            if fused:
+                nc.vector.tensor_tensor(
+                    out=y[:, :fused], in0=window.indirect(list_held[:, : fused // 16]), in1=og[:, :fused], op=ALU.add
+                )
+            nc.vector.tensor_tensor(out=y[:, fused:], in0=picked_held[:], in1=og[:, fused:], op=ALU.add)
             nc.sync.dma_start(out=out[k * P : (k + 1) * P, :], in_=y[:])
 
-        vt01 = sb("vt01", [P, 2, P, 2], F32)
-        turn((0, 1), vt01, nc.vector.tensor_copy)
-        og01 = sb("og01", [P, 2, J], F32)
-        gained(product("01", 2, vt01, sb("v_codes01", [P, 2 * P], U32)), og01, 2)
-        vt2 = sb("vt2", [P, 1, P, 2], F32)
-        turn((2,), vt2, nc.scalar.copy)
-        og2 = sb("og2", [P, 1, J], F32)
-        gained(product("2", 1, vt2, sb("v_codes2", [P, P], U32)), og2, 1)
-        vt3 = sb("vt3", [P, 1, P, 2], F32)
-        turn((3,), vt3, nc.scalar.copy)
-        merge(0, og01[:, 0, :], sb("y0", [P, J], F32))
-        merge(1, og01[:, 1, :], sb("y1", [P, J], F32))
-        o3 = product("3", 1, vt3, sb("v_codes3", [P, P], U32, tag="og01"))
-        merge(2, og2[:, 0, :], sb("y2", [P, J], F32))
-        og3 = sb("og3", [P, 1, J], F32, tag="og2")
-        gained(o3, og3, 1)
-        merge(3, og3[:, 0, :], sb("y3", [P, J], F32))
+        ogs = gained_products([(0, 1)]) + gained_products([(2,)]) + gained_products([(3,)])
+        for k in range(E // P):
+            merge(k, ogs[k], J // 2 if k == E // P - 1 else 0)

@@ -4,9 +4,13 @@ import concourse.mybir as mybir
 from concourse.masks import make_identity
 
 D, T, I, J, U, E, M = 512, 2048, 512, 256, 1024, 512, 1024
+FLOPS = 2 * (2 * D * I * J) + 2 * I * E * J
+
 P = 128
 PACK = 4
-FLOPS = 2 * D * I * J * 2 + 2 * I * E * J
+LIST_ROWS = 16
+HALVES = J // P
+E_TILES = E // P
 
 F32 = mybir.dt.float32
 BF16 = mybir.dt.bfloat16
@@ -37,10 +41,10 @@ def tile_attend_tab_larger_merge_kernel(
         ident = sb("ident", [P, P], F32)
         make_identity(nc, ident[:])
 
-        def load_pair(queue, name, src, half):
+        def load_pair(queue, name, src, pair):
             tile = sb(name, [P, 2 * U], F32)
             queue.dma_start(
-                out=tile[:], in_=src.rearrange("(p t) u -> p (t u)", t=PACK)[:, half * 2 * U : (half + 1) * 2 * U]
+                out=tile[:], in_=src.rearrange("(p t) u -> p (t u)", t=PACK)[:, pair * 2 * U : (pair + 1) * 2 * U]
             )
             return tile
 
@@ -53,46 +57,66 @@ def tile_attend_tab_larger_merge_kernel(
         nc.scalar.dma_start(
             out=key_words[:].bitcast(I32), in_=keys_words[0].rearrange("p n t -> p (n t)").bitcast(I32)
         )
-        notes_pairs = [load_pair(nc.scalar, "notes%d" % h, notes, h) for h in range(2)]
-        list_i = load_list("list_i", offs)
+        notes_pairs = [load_pair(nc.scalar, "notes%d" % pair, notes, pair) for pair in range(PACK // 2)]
+        list_tokens = load_list("list_tokens", offs)
         list_held = load_list("list_held", offs4)
         nc.sync.dma_start(out=gain_pool[0:1, :], in_=hgain[0:1, :])
-        for q in range(4):
+        for quadrant in range(4):
             nc.sync.dma_start(
-                out=key_bytes[32 * q : 32 * q + 4, :].bitcast(I32),
-                in_=keys_scales[0, 4 * q : 4 * q + 4, :].bitcast(I32),
+                out=key_bytes[32 * quadrant : 32 * quadrant + 4, :].bitcast(I32),
+                in_=keys_scales[0, 4 * quadrant : 4 * quadrant + 4, :].bitcast(I32),
             )
         list_notes = load_list("list_notes", offs2)
         row_factor = sb("row_factor", [P, PACK], F32)
         nc.sync.dma_start(out=row_factor[:], in_=rowf.rearrange("(p t) o -> p (t o)", t=PACK))
         list_users = load_list("list_users", offs3)
-        users_pairs = [load_pair(nc.sync, "users%d" % h, users2, h) for h in range(2)]
+        users_pairs = [load_pair(nc.sync, "users%d" % pair, users2, pair) for pair in range(PACK // 2)]
         vals_tiles = []
-        for k in range(E // P):
+        for k in range(E_TILES):
             tile = sb("vals%d" % k, [P, T], F32)
             nc.sync.dma_start(out=tile[:], in_=vals[k * P : (k + 1) * P, :])
             vals_tiles.append(tile)
         held_tiles = []
-        for k in range(E // P):
+        for k in range(E_TILES):
             tile = sb("held%d" % k, [P, M], F32)
             nc.sync.dma_start(out=tile[:], in_=held[k * P : (k + 1) * P, :])
             held_tiles.append(tile)
 
-        def quantised_columns(name, pairs, lst, on_scalar):
-            planes = sb(name + "_planes", [P, PACK, J], F32)
+        gain_row = sb("gain_row", [P, J], F32)
+        nc.scalar.activation(out=gain_row[:], in_=gain_pool[:].indirect(list_held[:]), func=COPY)
+        gain_cols = psum.tile([P, HALVES, P], F32, name="gain_cols")
+        for h in range(HALVES):
+            nc.tensor.transpose(gain_cols[:, h, :], gain_row[:, h * P : (h + 1) * P], ident[:])
+        gain_spread = sb("gain_spread", [P, HALVES, P], F32)
+        nc.scalar.copy(out=gain_spread[:], in_=gain_cols[:, :, 0:1].to_broadcast([P, HALVES, P]))
+        gain_rows = psum.tile([P, J], F32, name="gain_rows")
+        for h in range(HALVES):
+            nc.tensor.transpose(gain_rows[:, h * P : (h + 1) * P], gain_spread[:, h, :], ident[:])
+        gain = sb("gain", [P, J], F32)
+        nc.scalar.copy(out=gain[:], in_=gain_rows[:])
+
+        picked_words = sb("picked_words", [P, I], U32)
+        picked_bytes = sb("picked_bytes", [P, I], U8)
+        for picked, pool in ((picked_words, key_words), (picked_bytes, key_bytes)):
+            nc.vector.tensor_copy(
+                out=picked[:].rearrange("p (t s) -> p s t", t=PACK), in_=pool[:].indirect(list_tokens[:])
+            )
+
+        def quantised_columns(name, pairs, columns):
+            by_place = sb(name + "_by_place", [P, PACK, J], F32)
             for t in range(PACK):
-                window = pairs[t // 2][:, (t % 2) * U : (t % 2 + 1) * U].indirect(lst[:])
-                if t not in on_scalar:
-                    nc.vector.tensor_copy(out=planes[:, t, :], in_=window)
+                window = pairs[t // 2][:, (t % 2) * U : (t % 2 + 1) * U].indirect(columns[:])
+                if t % 2 == 0:
+                    nc.vector.tensor_copy(out=by_place[:, t, :], in_=window)
                 else:
-                    nc.scalar.activation(out=planes[:, t, :], in_=window, func=COPY)
+                    nc.scalar.activation(out=by_place[:, t, :], in_=window, func=COPY)
             woven = sb(name + "_woven", [P, J, PACK], BF16)
-            for h in range(2):
+            for h in range(HALVES):
                 cols = slice(h * P, (h + 1) * P)
-                nc.vector.tensor_copy(out=woven[:, cols, :], in_=planes[:, :, cols].rearrange("p t j -> p j t"))
+                nc.vector.tensor_copy(out=woven[:, cols, :], in_=by_place[:, :, cols].rearrange("p t j -> p j t"))
             codes = sb(name + "_codes", [P, J], U32)
             scales = sb(name + "_scales", [P, J], U8)
-            for h in range(2):
+            for h in range(HALVES):
                 cols = slice(h * P, (h + 1) * P)
                 nc.vector.quantize_mx(
                     out=codes[:, cols].bitcast(FP8X4),
@@ -101,15 +125,15 @@ def tile_attend_tab_larger_merge_kernel(
                 )
             return codes, scales
 
-        def table(name, codes, scales):
+        def key_products(name, codes, scales):
             banks = []
-            for h in range(2):
-                bank = psum.tile([P, PACK, P], F32, name="%s_bank%d" % (name, h), tag=name, bufs=2)
+            for h in range(HALVES):
+                bank = psum.tile([P, PACK, P], F32, name="%s_bank%d" % (name, h), tag=name, bufs=HALVES)
                 for t in range(PACK):
                     nc.tensor.matmul_mx(
                         out=bank[:, t, :],
-                        lhsT=kq[:, t * P : (t + 1) * P].bitcast(FP8X4),
-                        lhsT_scale=ks[:, t * P : (t + 1) * P],
+                        lhsT=picked_words[:, t * P : (t + 1) * P].bitcast(FP8X4),
+                        lhsT_scale=picked_bytes[:, t * P : (t + 1) * P],
                         rhs=codes[:, h * P : (h + 1) * P].bitcast(FP8X4),
                         rhs_scale=scales[:, h * P : (h + 1) * P],
                         start=True,
@@ -118,107 +142,89 @@ def tile_attend_tab_larger_merge_kernel(
                 banks.append(bank)
             return banks
 
-        gain_row = sb("gain_row", [P, J], F32)
-        nc.scalar.activation(out=gain_row[:], in_=gain_pool[:].indirect(list_held[:]), func=COPY)
-        gain_cols = psum.tile([P, 2, P], F32, name="gain_cols")
-        for h in range(2):
-            nc.tensor.transpose(gain_cols[:, h, :], gain_row[:, h * P : (h + 1) * P], ident[:])
-        gain_spread = sb("gain_spread", [P, 2, P], F32)
-        nc.scalar.copy(out=gain_spread[:], in_=gain_cols[:, :, 0:1].to_broadcast([P, 2, P]))
-        gain_rows = psum.tile([P, J], F32, name="gain_rows")
-        for h in range(2):
-            nc.tensor.transpose(gain_rows[:, h * P : (h + 1) * P], gain_spread[:, h, :], ident[:])
-        gain = sb("gain", [P, J], F32)
-        nc.scalar.copy(out=gain[:], in_=gain_rows[:])
-
-        kq = sb("kq", [P, I], U32)
-        ks = sb("ks", [P, I], U8)
-        nc.vector.tensor_copy(out=kq[:].rearrange("p (t s) -> p s t", t=PACK), in_=key_words[:].indirect(list_i[:]))
-        nc.vector.tensor_copy(out=ks[:].rearrange("p (t s) -> p s t", t=PACK), in_=key_bytes[:].indirect(list_i[:]))
-        notes_mx = quantised_columns("notes", notes_pairs, list_notes, (1, 3))
+        notes_mx = quantised_columns("notes", notes_pairs, list_notes)
         factor = sb("factor", [P, P, PACK], F32)
         nc.vector.tensor_copy(out=factor[:], in_=row_factor[:].unsqueeze(1).to_broadcast([P, P, PACK]))
 
-        g1_banks = table("notes", *notes_mx)
-        g1 = sb("g1", [P, 2, P, PACK], F32)
-        for h in range(2):
+        g1_banks = key_products("notes", *notes_mx)
+        g1 = sb("g1", [P, HALVES, P, PACK], F32)
+        for h in range(HALVES):
             nc.vector.tensor_copy(out=g1[:, h], in_=g1_banks[h][:].rearrange("p t j -> p j t"))
-        users_mx = quantised_columns("users", users_pairs, list_users, (1, 3))
-        g2_banks = table("users", *users_mx)
+        users_mx = quantised_columns("users", users_pairs, list_users)
+        g2_banks = key_products("users", *users_mx)
 
-        g0 = sb("g0", [P, 2, P, PACK], F32)
-        gr = [sb("gr%d" % h, [P, P, PACK], BF16) for h in range(2)]
-        for h in range(2):
+        g0 = sb("g0", [P, HALVES, P, PACK], F32)
+        gr1 = [sb("gr1_%d" % h, [P, P, PACK], BF16) for h in range(HALVES)]
+        for h in range(HALVES):
             nc.vector.tensor_tensor(
                 out=g0[:, h], in0=g2_banks[h][:].rearrange("p t j -> p j t"), in1=g1[:, h], op=ALU.max
             )
-        for h in range(2):
-            nc.vector.tensor_tensor(out=gr[h][:], in0=g0[:, h], in1=factor[:], op=ALU.mult)
-        gr_codes = sb("gr_codes", [P, J], U32)
-        gr_scales = sb("gr_scales", [P, J], U8)
-        for h in range(2):
+        for h in range(HALVES):
+            nc.vector.tensor_tensor(out=gr1[h][:], in0=g0[:, h], in1=factor[:], op=ALU.mult)
+        gr1_codes = sb("gr1_codes", [P, J], U32)
+        gr1_scales = sb("gr1_scales", [P, J], U8)
+        for h in range(HALVES):
             nc.vector.quantize_mx(
-                out=gr_codes[:, h * P : (h + 1) * P].bitcast(FP8X4),
-                scales=gr_scales[:, h * P : (h + 1) * P],
-                in_=gr[h][:].rearrange("p j t -> p (j t)"),
+                out=gr1_codes[:, h * P : (h + 1) * P].bitcast(FP8X4),
+                scales=gr1_scales[:, h * P : (h + 1) * P],
+                in_=gr1[h][:].rearrange("p j t -> p (j t)"),
             )
 
-        def turn(tiles, vt):
-            turned = psum.tile([P, len(tiles), 2, P], F32, name="turned%d" % tiles[0], tag="users", bufs=2)
+        def gained_products(tiles):
+            first, n = tiles[0], len(tiles)
+            turned = psum.tile([P, n, 2, P], F32, name="turned%d" % first, tag="users", bufs=HALVES)
             for a, k in enumerate(tiles):
-                picked = sb("picked%d" % k, [P, I], BF16)
-                nc.scalar.activation(out=picked[:], in_=vals_tiles[k][:].indirect(list_i[:]), func=COPY)
-                words = picked[:].bitcast(F32)
+                picked_vals = sb("picked_vals%d" % k, [P, I], BF16)
+                nc.scalar.activation(out=picked_vals[:], in_=vals_tiles[k][:].indirect(list_tokens[:]), func=COPY)
+                pair_words = picked_vals[:].bitcast(F32)
                 for u in range(2):
-                    nc.tensor.transpose(turned[:, a, u, :], words[:, u : I // 2 : 2], ident[:])
-            nc.vector.tensor_copy(out=vt, in_=turned[:].rearrange("p a u e -> p a e u"))
-
-        def gained_products(banks):
-            first = banks[0][0]
-            n = sum(len(tiles) for tiles in banks)
-            vt = sb("vt%d" % first, [P, n, P, 2], F32)
-            for tiles in banks:
-                turn(tiles, vt[:, tiles[0] - first : tiles[-1] + 1 - first])
-            v_codes = sb("v_codes%d" % first, [P, n * P], U32)
-            v_scales = sb("v_scales%d" % first, [P, n * P], U8)
+                    nc.tensor.transpose(turned[:, a, u, :], pair_words[:, u : I // 2 : 2], ident[:])
+            vt1 = sb("vt1_%d" % first, [P, n, P, 2], F32)
+            nc.vector.tensor_copy(out=vt1[:], in_=turned[:].rearrange("p a u e -> p a e u"))
+            vt1_codes = sb("vt1_codes%d" % first, [P, n * P], U32)
+            vt1_scales = sb("vt1_scales%d" % first, [P, n * P], U8)
             nc.vector.quantize_mx(
-                out=v_codes[:].bitcast(FP8X4),
-                scales=v_scales[:],
-                in_=vt[:].rearrange("p a e u -> p (a e u)").bitcast(BF16),
+                out=vt1_codes[:].bitcast(FP8X4),
+                scales=vt1_scales[:],
+                in_=vt1[:].rearrange("p a e u -> p (a e u)").bitcast(BF16),
             )
-            gained = []
-            for tiles in banks:
-                o = psum.tile([P, len(tiles), J], F32, name="o%d" % tiles[0], tag="notes", bufs=2)
-                for a, k in enumerate(tiles):
-                    cols = slice((k - first) * P, (k - first + 1) * P)
-                    nc.tensor.matmul_mx(
-                        out=o[:, a, :],
-                        lhsT=v_codes[:, cols].bitcast(FP8X4),
-                        lhsT_scale=v_scales[:, cols],
-                        rhs=gr_codes[:].bitcast(FP8X4),
-                        rhs_scale=gr_scales[:],
-                        start=True,
-                        stop=True,
-                    )
-                og = sb("og%d" % tiles[0], [P, len(tiles), J], F32)
-                nc.vector.tensor_tensor(
-                    out=og[:], in0=o[:], in1=gain[:].unsqueeze(1).to_broadcast([P, len(tiles), J]), op=ALU.mult
+            o = psum.tile([P, n, J], F32, name="o%d" % first, tag="notes", bufs=HALVES)
+            for a in range(n):
+                nc.tensor.matmul_mx(
+                    out=o[:, a, :],
+                    lhsT=vt1_codes[:, a * P : (a + 1) * P].bitcast(FP8X4),
+                    lhsT_scale=vt1_scales[:, a * P : (a + 1) * P],
+                    rhs=gr1_codes[:].bitcast(FP8X4),
+                    rhs_scale=gr1_scales[:],
+                    start=True,
+                    stop=True,
                 )
-                gained.extend(og[:, a, :] for a in range(len(tiles)))
-            return gained
+            gained = sb("gained%d" % first, [P, n, J], F32)
+            nc.vector.tensor_tensor(
+                out=gained[:], in0=o[:], in1=gain[:].unsqueeze(1).to_broadcast([P, n, J]), op=ALU.mult
+            )
+            return [gained[:, a, :] for a in range(n)]
 
-        def merge(k, og, fused):
-            y = sb("y%d" % k, [P, J], F32)
+        def merge(k, gained, fused, tag):
+            result = sb("result%d" % k, [P, J], F32, tag)
             picked_held = sb("picked_held%d" % k, [P, J - fused], F32)
             window = held_tiles[k][:]
-            nc.scalar.activation(out=picked_held[:], in_=window.indirect(list_held[:, fused // 16 :]), func=COPY)
+            nc.scalar.activation(
+                out=picked_held[:], in_=window.indirect(list_held[:, fused // LIST_ROWS :]), func=COPY
+            )
             if fused:
                 nc.vector.tensor_tensor(
-                    out=y[:, :fused], in0=window.indirect(list_held[:, : fused // 16]), in1=og[:, :fused], op=ALU.add
+                    out=result[:, :fused],
+                    in0=window.indirect(list_held[:, : fused // LIST_ROWS]),
+                    in1=gained[:, :fused],
+                    op=ALU.add,
                 )
-            nc.vector.tensor_tensor(out=y[:, fused:], in0=picked_held[:], in1=og[:, fused:], op=ALU.add)
-            nc.sync.dma_start(out=out[k * P : (k + 1) * P, :], in_=y[:])
+            nc.vector.tensor_tensor(out=result[:, fused:], in0=picked_held[:], in1=gained[:, fused:], op=ALU.add)
+            nc.sync.dma_start(out=out[k * P : (k + 1) * P, :], in_=result[:])
 
-        ogs = gained_products([(0, 1)]) + gained_products([(2,)]) + gained_products([(3,)])
-        for k in range(E // P):
-            merge(k, ogs[k], J // 2 if k == E // P - 1 else 0)
+        gained_tiles = gained_products((0, 1)) + gained_products((2,)) + gained_products((3,))
+
+        merge(0, gained_tiles[0], 0, None)
+        merge(1, gained_tiles[1], 0, "vt1_3")
+        merge(2, gained_tiles[2], 0, "gain")
+        merge(3, gained_tiles[3], J // 2, None)

from contextlib import ExitStack

import concourse.mybir as mybir
from concourse.masks import make_identity

D, T, I, J, U, E, M = 512, 2048, 512, 256, 1024, 512, 1024
FLOPS = 2 * (2 * D * I * J) + 2 * I * E * J

P = 128
PACK = 4
LIST_ROWS = 16
HALVES = J // P
E_TILES = E // P

F32 = mybir.dt.float32
BF16 = mybir.dt.bfloat16
I32 = mybir.dt.int32
U32 = mybir.dt.uint32
U16 = mybir.dt.uint16
U8 = mybir.dt.uint8
FP8X4 = mybir.dt.float8_e4m3fn_x4
COPY = mybir.ActivationFunctionType.Copy
ALU = mybir.AluOpType


def tile_attend_tab_larger_merge_kernel(
    tc, keys_words, keys_scales, notes, users2, rowf, vals, held, hgain, offs, offs2, offs3, offs4, out
):
    nc = tc.nc
    with ExitStack() as ctx:
        keep = ctx.enter_context(tc.tile_pool(name="keep", bufs=1))
        psum = ctx.enter_context(tc.psum_pool(name="psum", bufs=1))

        def sb(name, shape, dtype, tag=None):
            return keep.tile(shape, dtype, name=name, tag=tag or name, align_bytes=64)

        key_bytes = sb("key_bytes", [P, T], U8)
        nc.gpsimd.memset(key_bytes[:].bitcast(I32), 0)
        gain_pool = sb("gain_pool", [P, M], F32)
        nc.vector.memset(gain_pool[:], 0.0)
        ident = sb("ident", [P, P], F32)
        make_identity(nc, ident[:])

        def load_pair(queue, name, src, pair):
            tile = sb(name, [P, 2 * U], F32)
            queue.dma_start(
                out=tile[:], in_=src.rearrange("(p t) u -> p (t u)", t=PACK)[:, pair * 2 * U : (pair + 1) * 2 * U]
            )
            return tile

        def load_list(name, src):
            tile = sb(name, list(src.shape), U16)
            nc.sync.dma_start(out=tile[:], in_=src)
            return tile

        key_words = sb("key_words", [P, T], U32)
        nc.scalar.dma_start(
            out=key_words[:].bitcast(I32), in_=keys_words[0].rearrange("p n t -> p (n t)").bitcast(I32)
        )
        notes_pairs = [load_pair(nc.scalar, "notes%d" % pair, notes, pair) for pair in range(PACK // 2)]
        list_tokens = load_list("list_tokens", offs)
        list_held = load_list("list_held", offs4)
        nc.sync.dma_start(out=gain_pool[0:1, :], in_=hgain[0:1, :])
        for quadrant in range(4):
            nc.sync.dma_start(
                out=key_bytes[32 * quadrant : 32 * quadrant + 4, :].bitcast(I32),
                in_=keys_scales[0, 4 * quadrant : 4 * quadrant + 4, :].bitcast(I32),
            )
        list_notes = load_list("list_notes", offs2)
        row_factor = sb("row_factor", [P, PACK], F32)
        nc.sync.dma_start(out=row_factor[:], in_=rowf.rearrange("(p t) o -> p (t o)", t=PACK))
        list_users = load_list("list_users", offs3)
        users_pairs = [load_pair(nc.sync, "users%d" % pair, users2, pair) for pair in range(PACK // 2)]
        vals_tiles = []
        for k in range(E_TILES):
            tile = sb("vals%d" % k, [P, T], F32)
            nc.sync.dma_start(out=tile[:], in_=vals[k * P : (k + 1) * P, :])
            vals_tiles.append(tile)
        held_tiles = []
        for k in range(E_TILES):
            tile = sb("held%d" % k, [P, M], F32)
            nc.sync.dma_start(out=tile[:], in_=held[k * P : (k + 1) * P, :])
            held_tiles.append(tile)

        gain_row = sb("gain_row", [P, J], F32)
        nc.scalar.activation(out=gain_row[:], in_=gain_pool[:].indirect(list_held[:]), func=COPY)
        gain_cols = psum.tile([P, HALVES, P], F32, name="gain_cols")
        for h in range(HALVES):
            nc.tensor.transpose(gain_cols[:, h, :], gain_row[:, h * P : (h + 1) * P], ident[:])
        gain_spread = sb("gain_spread", [P, HALVES, P], F32)
        nc.scalar.copy(out=gain_spread[:], in_=gain_cols[:, :, 0:1].to_broadcast([P, HALVES, P]))
        gain_rows = psum.tile([P, J], F32, name="gain_rows")
        for h in range(HALVES):
            nc.tensor.transpose(gain_rows[:, h * P : (h + 1) * P], gain_spread[:, h, :], ident[:])
        gain = sb("gain", [P, J], F32)
        nc.scalar.copy(out=gain[:], in_=gain_rows[:])

        picked_words = sb("picked_words", [P, I], U32)
        picked_bytes = sb("picked_bytes", [P, I], U8)
        for picked, pool in ((picked_words, key_words), (picked_bytes, key_bytes)):
            nc.vector.tensor_copy(
                out=picked[:].rearrange("p (t s) -> p s t", t=PACK), in_=pool[:].indirect(list_tokens[:])
            )

        def quantised_columns(name, pairs, columns):
            by_place = sb(name + "_by_place", [P, PACK, J], F32)
            for t in range(PACK):
                window = pairs[t // 2][:, (t % 2) * U : (t % 2 + 1) * U].indirect(columns[:])
                if t % 2 == 0:
                    nc.vector.tensor_copy(out=by_place[:, t, :], in_=window)
                else:
                    nc.scalar.activation(out=by_place[:, t, :], in_=window, func=COPY)
            woven = sb(name + "_woven", [P, J, PACK], BF16)
            for h in range(HALVES):
                cols = slice(h * P, (h + 1) * P)
                nc.vector.tensor_copy(out=woven[:, cols, :], in_=by_place[:, :, cols].rearrange("p t j -> p j t"))
            codes = sb(name + "_codes", [P, J], U32)
            scales = sb(name + "_scales", [P, J], U8)
            for h in range(HALVES):
                cols = slice(h * P, (h + 1) * P)
                nc.vector.quantize_mx(
                    out=codes[:, cols].bitcast(FP8X4),
                    scales=scales[:, cols],
                    in_=woven[:, cols, :].rearrange("p j t -> p (j t)"),
                )
            return codes, scales

        def key_products(name, codes, scales):
            banks = []
            for h in range(HALVES):
                bank = psum.tile([P, PACK, P], F32, name="%s_bank%d" % (name, h), tag=name, bufs=HALVES)
                for t in range(PACK):
                    nc.tensor.matmul_mx(
                        out=bank[:, t, :],
                        lhsT=picked_words[:, t * P : (t + 1) * P].bitcast(FP8X4),
                        lhsT_scale=picked_bytes[:, t * P : (t + 1) * P],
                        rhs=codes[:, h * P : (h + 1) * P].bitcast(FP8X4),
                        rhs_scale=scales[:, h * P : (h + 1) * P],
                        start=True,
                        stop=True,
                    )
                banks.append(bank)
            return banks

        notes_mx = quantised_columns("notes", notes_pairs, list_notes)
        factor = sb("factor", [P, P, PACK], F32)
        nc.vector.tensor_copy(out=factor[:], in_=row_factor[:].unsqueeze(1).to_broadcast([P, P, PACK]))

        g1_banks = key_products("notes", *notes_mx)
        g1 = sb("g1", [P, HALVES, P, PACK], F32)
        for h in range(HALVES):
            nc.vector.tensor_copy(out=g1[:, h], in_=g1_banks[h][:].rearrange("p t j -> p j t"))
        users_mx = quantised_columns("users", users_pairs, list_users)
        g2_banks = key_products("users", *users_mx)

        g0 = sb("g0", [P, HALVES, P, PACK], F32)
        gr1 = [sb("gr1_%d" % h, [P, P, PACK], BF16) for h in range(HALVES)]
        for h in range(HALVES):
            nc.vector.tensor_tensor(
                out=g0[:, h], in0=g2_banks[h][:].rearrange("p t j -> p j t"), in1=g1[:, h], op=ALU.max
            )
        for h in range(HALVES):
            nc.vector.tensor_tensor(out=gr1[h][:], in0=g0[:, h], in1=factor[:], op=ALU.mult)
        gr1_codes = sb("gr1_codes", [P, J], U32)
        gr1_scales = sb("gr1_scales", [P, J], U8)
        for h in range(HALVES):
            nc.vector.quantize_mx(
                out=gr1_codes[:, h * P : (h + 1) * P].bitcast(FP8X4),
                scales=gr1_scales[:, h * P : (h + 1) * P],
                in_=gr1[h][:].rearrange("p j t -> p (j t)"),
            )

        def gained_products(tiles):
            first, n = tiles[0], len(tiles)
            turned = psum.tile([P, n, 2, P], F32, name="turned%d" % first, tag="users", bufs=HALVES)
            for a, k in enumerate(tiles):
                picked_vals = sb("picked_vals%d" % k, [P, I], BF16)
                nc.scalar.activation(out=picked_vals[:], in_=vals_tiles[k][:].indirect(list_tokens[:]), func=COPY)
                pair_words = picked_vals[:].bitcast(F32)
                for u in range(2):
                    nc.tensor.transpose(turned[:, a, u, :], pair_words[:, u : I // 2 : 2], ident[:])
            vt1 = sb("vt1_%d" % first, [P, n, P, 2], F32)
            nc.vector.tensor_copy(out=vt1[:], in_=turned[:].rearrange("p a u e -> p a e u"))
            vt1_codes = sb("vt1_codes%d" % first, [P, n * P], U32)
            vt1_scales = sb("vt1_scales%d" % first, [P, n * P], U8)
            nc.vector.quantize_mx(
                out=vt1_codes[:].bitcast(FP8X4),
                scales=vt1_scales[:],
                in_=vt1[:].rearrange("p a e u -> p (a e u)").bitcast(BF16),
            )
            o = psum.tile([P, n, J], F32, name="o%d" % first, tag="notes", bufs=HALVES)
            for a in range(n):
                nc.tensor.matmul_mx(
                    out=o[:, a, :],
                    lhsT=vt1_codes[:, a * P : (a + 1) * P].bitcast(FP8X4),
                    lhsT_scale=vt1_scales[:, a * P : (a + 1) * P],
                    rhs=gr1_codes[:].bitcast(FP8X4),
                    rhs_scale=gr1_scales[:],
                    start=True,
                    stop=True,
                )
            gained = sb("gained%d" % first, [P, n, J], F32)
            nc.vector.tensor_tensor(
                out=gained[:], in0=o[:], in1=gain[:].unsqueeze(1).to_broadcast([P, n, J]), op=ALU.mult
            )
            return [gained[:, a, :] for a in range(n)]

        def merge(k, gained, fused, tag):
            result = sb("result%d" % k, [P, J], F32, tag)
            picked_held = sb("picked_held%d" % k, [P, J - fused], F32)
            window = held_tiles[k][:]
            nc.scalar.activation(
                out=picked_held[:], in_=window.indirect(list_held[:, fused // LIST_ROWS :]), func=COPY
            )
            if fused:
                nc.vector.tensor_tensor(
                    out=result[:, :fused],
                    in0=window.indirect(list_held[:, : fused // LIST_ROWS]),
                    in1=gained[:, :fused],
                    op=ALU.add,
                )
            nc.vector.tensor_tensor(out=result[:, fused:], in0=picked_held[:], in1=gained[:, fused:], op=ALU.add)
            nc.sync.dma_start(out=out[k * P : (k + 1) * P, :], in_=result[:])

        gained_tiles = gained_products((0, 1)) + gained_products((2,)) + gained_products((3,))

        merge(0, gained_tiles[0], 0, None)
        merge(1, gained_tiles[1], 0, "vt1_3")
        merge(2, gained_tiles[2], 0, "gain")
        merge(3, gained_tiles[3], J // 2, None)
